import numpy as np
import ml_dtypes


def mxq(x, axis, fmt="e4m3"):
    dtype, down = {"e4m3": (ml_dtypes.float8_e4m3fn, 7), "e5m2": (ml_dtypes.float8_e5m2, 14)}[fmt]
    v = np.moveaxis(np.asarray(x, np.float32).astype(ml_dtypes.bfloat16).astype(np.float64), axis, -1)
    blocks = v.reshape(v.shape[:-1] + (-1, 32))
    amax = np.abs(blocks).max(-1, keepdims=True)
    byte = np.maximum(np.where(amax > 0, np.frexp(amax)[1] - 1 + 127, 0) - down, 1)
    scale = np.exp2(byte - 127.0)
    codes = (blocks / scale).astype(np.float32).astype(dtype).astype(np.float64)
    return np.moveaxis((codes * scale).reshape(v.shape), -1, axis)


WIDE = False


def mx_kscale(k):
    if not WIDE:
        return np.ones(k)
    levels = np.array([10, -10, 5, -5, 0])
    if k % 512:
        return np.exp2(np.random.permutation(np.resize(levels, k // 32))).repeat(32)
    a = np.empty((k // 512, 16))
    for p in range(k // 512):
        a[p, :8] = np.random.permutation(np.resize(levels, 8))
        for g in range(8):
            far = levels[np.abs(levels - a[p, g]) >= 10]
            a[p, g + 8] = far[np.random.randint(len(far))]
    return np.exp2(a.ravel()).repeat(32)


def f64(x):
    return np.asarray(x).astype(np.float64)


def striped(idx):
    return np.tile(idx.reshape(-1, 16).T, (8, 1)).astype(np.uint16)


def unstriped(offs):
    return offs[:16].T.reshape(-1).astype(np.int64)


E2M1 = np.array([0.0, 0.5, 1.0, 1.5, 2.0, 3.0, 4.0, 6.0, -0.0, -0.5, -1.0, -1.5, -2.0, -3.0, -4.0, -6.0])


def pack_weight(w, fmt):
    k, n = w.shape
    w = f64(np.asarray(w, np.float32).astype(ml_dtypes.bfloat16)).reshape(k // 32, 32, n)
    amax = np.abs(w).max(1)
    if fmt == "e4m3":
        byte = np.frexp(amax)[1] - 1 + 127 - 7
    else:
        mant, ex = np.frexp(amax / 6.0)
        byte = np.where(mant > 0.5, ex, ex - 1) + 127
    byte = np.clip(np.where(amax > 0, byte, 1), 1, 254)
    scaled = (w * np.exp2(127.0 - byte)[:, None, :]).reshape(k, n).astype(np.float32)
    by_word = np.ascontiguousarray(scaled.reshape(k // 512, 128, 4, n).transpose(0, 1, 3, 2))
    if fmt == "e4m3":
        words = by_word.astype(ml_dtypes.float8_e4m3fn).view(np.uint8)
    else:
        c = by_word.astype(ml_dtypes.float4_e2m1fn).view(np.uint8) & 0xF
        words = (c[..., 0::2] | (c[..., 1::2] << 4)).reshape(k // 512, 128, 2 * n)
    return np.ascontiguousarray(words), np.ascontiguousarray(byte.astype(np.uint8).reshape(k // 512, 16, n))


def unpack_weight(words, scales, fmt):
    g, _, n = scales.shape
    words = np.ascontiguousarray(words).reshape(g, 128, n, -1)
    if fmt == "e4m3":
        vals = words.view(ml_dtypes.float8_e4m3fn).astype(np.float64)
    else:
        nib = np.empty((g, 128, n, 4), np.uint8)
        nib[..., 0::2] = words & 0xF
        nib[..., 1::2] = words >> 4
        vals = E2M1[nib]
    vals = vals * np.repeat(np.exp2(scales.astype(np.float64) - 127.0), 8, axis=1)[..., None]
    return vals.transpose(0, 1, 3, 2).reshape(g * 512, n)


def gelu(v):
    return 0.5 * v * (1.0 + np.tanh(np.sqrt(2.0 / np.pi) * (v + 0.044715 * v**3)))


def bf(x):
    return np.asarray(x, np.float32).astype(ml_dtypes.bfloat16)


def planes(Y):
    n, m = Y.shape
    b = f64(bf(Y)).reshape(n // 32, 32, m)
    amax = np.abs(b).max(1)
    byte = np.clip(np.where(amax > 0, np.frexp(amax)[1] - 1 + 127 - 7, 1), 1, 254)
    codes = (b * np.exp2(127.0 - byte)[:, None, :]).reshape(n, m).astype(np.float32).astype(ml_dtypes.float8_e4m3fn).view(np.uint8)
    words = codes.reshape(n // 512, 128, 4, m).transpose(0, 1, 3, 2)
    return np.ascontiguousarray(words), np.ascontiguousarray(byte.astype(np.uint8).reshape(n // 512, 16, m))


K, H, T, S, T2, P = 1536, 1024, 2048, 512, 1024, 512

def setup_inputs():
    n = np.random.standard_normal
    s = mx_kscale(K)[:, None]
    u = mx_kscale(H)[:, None]
    size = 0.4 * np.exp(0.8 * n(H))
    d = {}
    d["tab_words"], d["tab_scales"] = pack_weight(n((K, T)) * s, "e4m3")
    d["offs"] = striped(np.random.permutation(T)[:S])
    d["w1_words"], d["w1_scales"] = pack_weight(1.5 * n((K, H)) / K**0.5 / s, "e2m1")
    d["texture"] = (n((H, S)) * u).astype(np.float32)
    d["page0"] = (n((H, T2)) * u).astype(np.float32)
    d["wgs"] = np.exp(0.3 * n((128, S))).astype(np.float32)
    d["offs2"] = striped(np.random.permutation(T2)[:S])
    d["dn"] = (np.random.uniform(1.2, 2.4, H) / u[:, 0]).astype(np.float32)
    d["offs3"] = striped(np.random.permutation(T2)[:P])
    d["up"] = (np.exp(0.3 * n(H)) * u[:, 0]).astype(np.float32)
    d["w2"] = (n((H, H)) / H**0.5 / u * size[None, :]).astype(np.float32)
    d["bulk"] = (n((H, P)) * size[:, None]).astype(np.float32)
    d["offs4"] = striped(np.random.permutation(T2)[:P])
    return d

def reference(tab_words, tab_scales, offs, w1_words, w1_scales, texture, page0, wgs, offs2, dn, offs3, up, w2, bulk, offs4):
    v = unpack_weight(tab_words, tab_scales, "e4m3")[:, unstriped(offs)]
    w1 = unpack_weight(w1_words, w1_scales, "e2m1")
    h = np.tanh(w1.T @ v) * f64(texture)
    page = f64(page0).copy()
    page[:, unstriped(offs2)] = np.tile(f64(wgs), (H // 128, 1)) * h
    page = f64(dn)[:, None] * page
    x = page[:, unstriped(offs3)]
    x = x / (1.0 + np.exp(-x))
    xq = mxq(f64(up)[:, None] * x, 0, "e4m3")
    w2q = mxq(f64(w2), 0, "e4m3")
    firm = (w2q.T @ xq) + f64(bulk)
    earlier = page[:, unstriped(offs4)]
    y = firm * earlier
    words, scales = planes(y)
    return y, words, scales

@@ -1,0 +1,243 @@
+from contextlib import ExitStack
+
+import concourse.mybir as mybir
+
+K, H, T, S, T2, PICK = 1536, 1024, 2048, 512, 1024, 512
+FLOPS = 2 * K * H * S + 2 * H * H * PICK
+
+F32 = mybir.dt.float32
+BF16 = mybir.dt.bfloat16
+I32 = mybir.dt.int32
+U32 = mybir.dt.uint32
+U16 = mybir.dt.uint16
+U8 = mybir.dt.uint8
+FP8X4 = mybir.dt.float8_e4m3fn_x4
+FP4X4 = mybir.dt.float4_e2m1fn_x4
+ACT = mybir.ActivationFunctionType
+MULT = mybir.AluOpType.mult
+ADD = mybir.AluOpType.add
+
+P = 128
+PACK = 4
+GROUP = P * PACK
+PASSES = K // GROUP
+GROUPS = H // GROUP
+SLICES = GROUPS * PACK
+QUADS = 4
+QUAD = P // QUADS
+SPARE = QUAD - 4 * PASSES
+SHIFT_ROWS = P - QUAD + 4
+
+
+def tile_list_foam_slice_firmness_kernel(
+    tc, tab_words, tab_scales, offs, w1_words, w1_scales, texture, page0, wgs, offs2, dn, offs3, up, w2, bulk, offs4,
+    out_0, out_1, out_2,
+):
+    nc = tc.nc
+
+    def dealt(rows, g):
+        return rows[g * GROUP : (g + 1) * GROUP, :].rearrange("(p t) j -> p t j", t=PACK)
+
+    with ExitStack() as ctx:
+        keep = ctx.enter_context(tc.tile_pool(name="keep", bufs=1))
+        ring = ctx.enter_context(tc.tile_pool(name="ring", bufs=3))
+        psum = ctx.enter_context(tc.psum_pool(name="psum", bufs=1))
+
+        list1 = keep.tile([P, S // 16], U16, name="list1")
+        list2 = keep.tile([P, S // 16], U16, name="list2")
+        list3 = keep.tile([P, PICK // 16], U16, name="list3")
+        list4 = keep.tile([P, PICK // 16], U16, name="list4")
+
+        tab_w = [keep.tile([P, T], I32, name=f"tab_w{a}", align_bytes=64) for a in range(PASSES)]
+        tab_s = keep.tile([P, T], U8, name="tab_s", align_bytes=64)
+        v_w = [keep.tile([P, S], U32, name=f"v_w{a}", align_bytes=64) for a in range(PASSES)]
+        v_s = [keep.tile([P, S], U8, name=f"v_s{a}", align_bytes=64) for a in range(PASSES)]
+        w1_raw = [keep.tile([P, PASSES, GROUP], U16, name=f"w1_raw{g}", align_bytes=64) for g in range(GROUPS)]
+        w1_w = [keep.tile([P, PACK, PASSES, P], U16, name=f"w1_w{g}", align_bytes=64) for g in range(GROUPS)]
+        w1_sraw = keep.tile([P, PASSES, H], U8, name="w1_sraw", align_bytes=64)
+        w1_s = [keep.tile([P, PACK, PASSES, P], U8, name=f"w1_s{g}", align_bytes=64) for g in range(GROUPS)]
+        tex = [keep.tile([P, PACK, S], F32, name=f"tex{g}", tag=f"rows{g}") for g in range(GROUPS)]
+        gain = keep.tile([P, PACK, S], F32, name="gain")
+        page = [keep.tile([P, T2], F32, name=f"page{s}") for s in range(SLICES)]
+        entry = [keep.tile([P, S], F32, name=f"entry{s}", tag=f"entry{s}", align_bytes=64) for s in range(SLICES)]
+        dn_t = keep.tile([P, GROUPS, PACK], F32, name="dn_t")
+        up_t = keep.tile([P, GROUPS, PACK], F32, name="up_t")
+        w2_raw = [[keep.tile([P, PACK, GROUP], F32, name=f"w2_raw{b}{g}") for g in range(GROUPS)] for b in range(GROUPS)]
+        w2_b = [[keep.tile([P, PACK * GROUP], BF16, name=f"w2_b{b}{g}", align_bytes=64) for g in range(GROUPS)] for b in range(GROUPS)]
+        w2_w = keep.tile([P, GROUPS, H], U32, name="w2_w", align_bytes=64)
+        x_b = [keep.tile([P, PICK, PACK], BF16, name=f"x_b{b}", align_bytes=64) for b in range(GROUPS)]
+        x_w = [keep.tile([P, PICK], U32, name=f"x_w{b}", align_bytes=64) for b in range(GROUPS)]
+        x_s = [keep.tile([P, PICK], U8, name=f"x_s{b}", align_bytes=64) for b in range(GROUPS)]
+        firm = [keep.tile([P, PACK, PICK], F32, name=f"firm{g}") for g in range(GROUPS)]
+        y_b = [keep.tile([P, PICK * PACK], BF16, name=f"y_b{g}", align_bytes=64) for g in range(GROUPS)]
+        y_w = [keep.tile([P, PICK], U32, name=f"y_w{g}", align_bytes=64) for g in range(GROUPS)]
+        y_s = [keep.tile([P, PICK], U8, name=f"y_s{g}", align_bytes=64) for g in range(GROUPS)]
+
+        nc.vector.memset(w1_sraw[:].rearrange("p a c -> p (a c)").bitcast(I32), 0)
+        for q in range(QUADS):
+            nc.vector.memset(tab_s[QUAD * q : QUAD * q + SPARE, :].bitcast(I32), 0)
+        for a in range(PASSES):
+            nc.vector.memset(v_s[a][:].bitcast(I32), 0)
+        for q in range(QUADS):
+            nc.scalar.dma_start(
+                out=tab_s[QUAD * q + SPARE : QUAD * (q + 1), :].bitcast(I32),
+                in_=tab_scales.bitcast(I32)[:, 4 * q : 4 * q + 4, :],
+            )
+        for q in range(QUADS):
+            nc.gpsimd.dma_start(
+                out=w1_sraw[QUAD * q : QUAD * q + 4, :, :].bitcast(I32),
+                in_=w1_scales.bitcast(I32)[:, 4 * q : 4 * q + 4, :].rearrange("a r w -> r a w"),
+            )
+
+        def load_tab(a):
+            nc.sync.dma_start(out=tab_w[a][:], in_=tab_words[a].rearrange("p t i -> p (t i)").bitcast(I32))
+
+        def load_w1(g):
+            half = GROUP // 2
+            nc.sync.dma_start(
+                out=w1_raw[g][:].bitcast(I32),
+                in_=w1_words.bitcast(I32)[:, :, g * half : (g + 1) * half].rearrange("a p w -> p a w"),
+            )
+
+        def load_texture(s):
+            g, t = divmod(s, PACK)
+            nc.sync.dma_start(out=tex[g][:, t, :], in_=dealt(texture, g)[:, t, :])
+
+        def load_gain(t0, t1):
+            rows = wgs.rearrange("(m t) j -> m t j", t=PACK)[:, t0:t1, :]
+            for q in (0, 2, 1, 3):
+                nc.sync.dma_start(out=gain[QUAD * q : QUAD * (q + 1), t0:t1, :], in_=rows)
+
+        def load_page(s):
+            g, t = divmod(s, PACK)
+            nc.sync.dma_start(out=page[s][:], in_=dealt(page0, g)[:, t, :])
+
+        def load_w2(b, g):
+            nc.sync.dma_start(out=w2_raw[b][g][:], in_=dealt(w2, b)[:, :, g * GROUP : (g + 1) * GROUP])
+
+        def load_bulk(g):
+            nc.sync.dma_start(out=firm[g][:], in_=dealt(bulk, g))
+
+        load_tab(0)
+        nc.sync.dma_start(list1[:], offs)
+        load_tab(1)
+        load_w1(0)
+        load_tab(2)
+        load_texture(0)
+        load_gain(0, 1)
+        load_page(0)
+        nc.sync.dma_start(list2[:], offs2)
+        nc.sync.dma_start(list3[:], offs3)
+        load_texture(1)
+        load_gain(1, 2)
+        load_w1(1)
+        nc.sync.dma_start(out=dn_t[:], in_=dn.rearrange("(g p t) -> p g t", g=GROUPS, t=PACK))
+        load_page(1)
+        nc.sync.dma_start(out=up_t[:], in_=up.rearrange("(g p t) -> p g t", g=GROUPS, t=PACK))
+        load_gain(2, 4)
+        nc.sync.dma_start(list4[:], offs4)
+        chunks = [(b, g) for g in range(GROUPS) for b in range(GROUPS)]
+        for s in range(2, SLICES):
+            load_texture(s)
+            load_page(s)
+            if s - 2 < len(chunks):
+                load_w2(*chunks[s - 2])
+            else:
+                load_bulk(s - 2 - len(chunks))
+
+        picked_s = keep.tile([P, S], U8, name="picked_s", align_bytes=64)
+        nc.vector.tensor_copy(out=picked_s[:], in_=tab_s[:].indirect(list1[:]))
+        for a in range(PASSES):
+            first = SPARE + 4 * a
+            nc.gpsimd.dma_start(
+                out=v_s[a][0:SHIFT_ROWS, :].bitcast(I32), in_=picked_s[first : first + SHIFT_ROWS, :].bitcast(I32)
+            )
+        for g in range(GROUPS):
+            nc.vector.tensor_copy(
+                out=w1_s[g][:],
+                in_=w1_sraw[:, :, g * GROUP : (g + 1) * GROUP].rearrange("p a (m t) -> p t a m", t=PACK),
+            )
+        for a in range(PASSES):
+            nc.vector.tensor_copy(out=v_w[a][:], in_=tab_w[a][:].bitcast(U32).indirect(list1[:]))
+
+        for g in range(GROUPS):
+            nc.scalar.copy(out=w1_w[g][:], in_=w1_raw[g][:].rearrange("p a (m t) -> p t a m", t=PACK))
+            for t in range(PACK):
+                s = g * PACK + t
+                acc = psum.tile([P, S], F32, name=f"acc{s}", tag=f"bank{s}")
+                for a in range(PASSES):
+                    nc.tensor.matmul_mx(
+                        out=acc[:],
+                        lhsT=w1_w[g][:, t, a, :].bitcast(FP4X4),
+                        lhsT_scale=w1_s[g][:, t, a, :],
+                        rhs=v_w[a][:].bitcast(FP8X4),
+                        rhs_scale=v_s[a][:],
+                        start=(a == 0),
+                        stop=(a == PASSES - 1),
+                    )
+                nc.scalar.activation(out=entry[s][:], in_=acc[:], func=ACT.Tanh)
+
+        for s in range(SLICES):
+            g, t = divmod(s, PACK)
+            if 0 <= s - 3 < len(chunks):
+                b2, g2 = chunks[s - 3]
+                nc.scalar.copy(
+                    out=w2_b[b2][g2][:].rearrange("p (t m i) -> p m i t", t=PACK, i=PACK),
+                    in_=w2_raw[b2][g2][:].rearrange("p i (m t) -> p m i t", t=PACK),
+                )
+            nc.gpsimd.tensor_tensor(out=tex[g][:, t, :], in0=tex[g][:, t, :], in1=gain[:, t, :], op=MULT)
+            engine = nc.vector if s == 0 else nc.gpsimd
+            engine.tensor_tensor(out=entry[s][:], in0=entry[s][:], in1=tex[g][:, t, :], op=MULT)
+            nc.vector.tensor_copy(out=page[s][:].indirect(list2[:]), in_=entry[s][:])
+            reread = ring.tile([P, PICK], F32, name="reread")
+            nc.vector.tensor_copy(out=reread[:], in_=page[s][:].indirect(list3[:]))
+            nc.scalar.activation(out=reread[:], in_=reread[:], func=ACT.Silu, scale=dn_t[:, g, t : t + 1])
+            nc.scalar.activation(out=x_b[g][:, :, t], in_=reread[:], func=ACT.Copy, scale=up_t[:, g, t : t + 1])
+            if t == PACK - 1:
+                nc.vector.quantize_mx(
+                    out=x_w[g][:].bitcast(FP8X4), scales=x_s[g][:], in_=x_b[g][:].rearrange("p j t -> p (j t)")
+                )
+
+        w2_s = keep.tile([P, GROUPS, H], U8, name="w2_s", tag=f"entry{SLICES - 1}", align_bytes=64)
+        for b, g in chunks:
+            cols = slice(g * GROUP, (g + 1) * GROUP)
+            nc.vector.quantize_mx(out=w2_w[:, b, cols].bitcast(FP8X4), scales=w2_s[:, b, cols], in_=w2_b[b][g][:])
+
+        for g in range(GROUPS):
+            y = keep.tile([P, PACK, PICK], F32, name=f"y{g}", tag=f"rows{g}")
+            for t in range(PACK):
+                s = g * PACK + t
+                cols = slice(s * P, (s + 1) * P)
+                scale = dn_t[:, g, t : t + 1]
+                nc.gpsimd.tensor_scalar(
+                    out=firm[g][:, t, :], in0=firm[g][:, t, :], scalar1=scale, scalar2=0.0, op0=MULT, op1=ADD
+                )
+                acc = psum.tile([P, PICK], F32, name=f"sum{s}", tag=f"bank{s}")
+                for b in range(GROUPS):
+                    nc.tensor.matmul_mx(
+                        out=acc[:],
+                        lhsT=w2_w[:, b, cols].bitcast(FP8X4),
+                        lhsT_scale=w2_s[:, b, cols],
+                        rhs=x_w[b][:].bitcast(FP8X4),
+                        rhs_scale=x_s[b][:],
+                        start=(b == 0),
+                        stop=(b == GROUPS - 1),
+                    )
+                nc.vector.scalar_tensor_tensor(
+                    out=firm[g][:, t, :], in0=acc[:], scalar=scale, in1=firm[g][:, t, :], op0=MULT, op1=ADD
+                )
+                nc.vector.tensor_tensor(out=y[:, t, :], in0=page[s][:].indirect(list4[:]), in1=firm[g][:, t, :], op=MULT)
+                nc.sync.dma_start(out=dealt(out_0, g)[:, t, :], in_=y[:, t, :])
+            rounded = y_b[g][:].rearrange("p (c i t) -> p c t i", i=4, t=PACK)
+            exact = y[:].rearrange("p t (c i) -> p c t i", i=4)
+            if g == 0:
+                nc.scalar.copy(out=rounded, in_=exact)
+            else:
+                nc.vector.tensor_copy(out=rounded, in_=exact)
+            nc.vector.quantize_mx(out=y_w[g][:].bitcast(FP8X4), scales=y_s[g][:], in_=y_b[g][:])
+            nc.sync.dma_start(out=out_1[g].rearrange("p m t -> p (m t)").bitcast(I32), in_=y_w[g][:].bitcast(I32))
+            for q in range(QUADS):
+                queue = nc.scalar if q % 2 else nc.sync
+                queue.dma_start(
+                    out=out_2[g].bitcast(I32)[4 * q : 4 * q + 4, :], in_=y_s[g][QUAD * q : QUAD * q + 4, :].bitcast(I32)
+                )

@@ -1,6 +1,7 @@
 from contextlib import ExitStack
 
 import concourse.mybir as mybir
+from concourse.masks import make_identity
 
 K, H, T, S, T2, PICK = 1536, 1024, 2048, 512, 1024, 512
 FLOPS = 2 * K * H * S + 2 * H * H * PICK
@@ -23,10 +24,10 @@ GROUP = P * PACK
 PASSES = K // GROUP
 GROUPS = H // GROUP
 SLICES = GROUPS * PACK
+BLOCKS = S // P
+VECTOR_RUNS = 80
 QUADS = 4
 QUAD = P // QUADS
-SPARE = QUAD - 4 * PASSES
-SHIFT_ROWS = P - QUAD + 4
 
 
 def tile_list_foam_slice_firmness_kernel(
@@ -40,7 +41,8 @@ def tile_list_foam_slice_firmness_kernel(
 
     with ExitStack() as ctx:
         keep = ctx.enter_context(tc.tile_pool(name="keep", bufs=1))
-        ring = ctx.enter_context(tc.tile_pool(name="ring", bufs=3))
+        ring = ctx.enter_context(tc.tile_pool(name="ring", bufs=SLICES))
+        pair = ctx.enter_context(tc.tile_pool(name="pair", bufs=1))
         psum = ctx.enter_context(tc.psum_pool(name="psum", bufs=1))
 
         list1 = keep.tile([P, S // 16], U16, name="list1")
@@ -49,45 +51,38 @@ def tile_list_foam_slice_firmness_kernel(
         list4 = keep.tile([P, PICK // 16], U16, name="list4")
 
         tab_w = [keep.tile([P, T], I32, name=f"tab_w{a}", align_bytes=64) for a in range(PASSES)]
-        tab_s = keep.tile([P, T], U8, name="tab_s", align_bytes=64)
-        v_w = [keep.tile([P, S], U32, name=f"v_w{a}", align_bytes=64) for a in range(PASSES)]
+        tab_s = keep.tile([P, PASSES, T], U8, name="tab_s", align_bytes=64)
         v_s = [keep.tile([P, S], U8, name=f"v_s{a}", align_bytes=64) for a in range(PASSES)]
-        w1_raw = [keep.tile([P, PASSES, GROUP], U16, name=f"w1_raw{g}", align_bytes=64) for g in range(GROUPS)]
-        w1_w = [keep.tile([P, PACK, PASSES, P], U16, name=f"w1_w{g}", align_bytes=64) for g in range(GROUPS)]
-        w1_sraw = keep.tile([P, PASSES, H], U8, name="w1_sraw", align_bytes=64)
-        w1_s = [keep.tile([P, PACK, PASSES, P], U8, name=f"w1_s{g}", align_bytes=64) for g in range(GROUPS)]
+        w1_w = [keep.tile([P, PASSES, GROUP], U16, name=f"w1_w{g}", align_bytes=64) for g in range(GROUPS)]
+        w1_s = keep.tile([P, PASSES, H], U8, name="w1_s", align_bytes=64)
+        bent = [keep.tile([P, BLOCKS, PACK, P], F32, name=f"bent{g}") for g in range(GROUPS)]
+        ident = keep.tile([P, P], F32, name="ident")
         tex = [keep.tile([P, PACK, S], F32, name=f"tex{g}", tag=f"rows{g}") for g in range(GROUPS)]
         gain = keep.tile([P, PACK, S], F32, name="gain")
         page = [keep.tile([P, T2], F32, name=f"page{s}") for s in range(SLICES)]
-        entry = [keep.tile([P, S], F32, name=f"entry{s}", tag=f"entry{s}", align_bytes=64) for s in range(SLICES)]
         dn_t = keep.tile([P, GROUPS, PACK], F32, name="dn_t")
         up_t = keep.tile([P, GROUPS, PACK], F32, name="up_t")
         w2_raw = [[keep.tile([P, PACK, GROUP], F32, name=f"w2_raw{b}{g}") for g in range(GROUPS)] for b in range(GROUPS)]
-        w2_b = [[keep.tile([P, PACK * GROUP], BF16, name=f"w2_b{b}{g}", align_bytes=64) for g in range(GROUPS)] for b in range(GROUPS)]
+        w2_b = [[keep.tile([P, PACK * GROUP], BF16, name=f"w2_b{b}{g}", tag=f"rounded{b}{g}", align_bytes=64) for g in range(GROUPS)] for b in range(GROUPS)]
         w2_w = keep.tile([P, GROUPS, H], U32, name="w2_w", align_bytes=64)
         x_b = [keep.tile([P, PICK, PACK], BF16, name=f"x_b{b}", align_bytes=64) for b in range(GROUPS)]
         x_w = [keep.tile([P, PICK], U32, name=f"x_w{b}", align_bytes=64) for b in range(GROUPS)]
         x_s = [keep.tile([P, PICK], U8, name=f"x_s{b}", align_bytes=64) for b in range(GROUPS)]
         firm = [keep.tile([P, PACK, PICK], F32, name=f"firm{g}") for g in range(GROUPS)]
-        y_b = [keep.tile([P, PICK * PACK], BF16, name=f"y_b{g}", align_bytes=64) for g in range(GROUPS)]
         y_w = [keep.tile([P, PICK], U32, name=f"y_w{g}", align_bytes=64) for g in range(GROUPS)]
         y_s = [keep.tile([P, PICK], U8, name=f"y_s{g}", align_bytes=64) for g in range(GROUPS)]
 
-        nc.vector.memset(w1_sraw[:].rearrange("p a c -> p (a c)").bitcast(I32), 0)
-        for q in range(QUADS):
-            nc.vector.memset(tab_s[QUAD * q : QUAD * q + SPARE, :].bitcast(I32), 0)
-        for a in range(PASSES):
-            nc.vector.memset(v_s[a][:].bitcast(I32), 0)
-        for q in range(QUADS):
-            nc.scalar.dma_start(
-                out=tab_s[QUAD * q + SPARE : QUAD * (q + 1), :].bitcast(I32),
-                in_=tab_scales.bitcast(I32)[:, 4 * q : 4 * q + 4, :],
-            )
-        for q in range(QUADS):
-            nc.gpsimd.dma_start(
-                out=w1_sraw[QUAD * q : QUAD * q + 4, :, :].bitcast(I32),
-                in_=w1_scales.bitcast(I32)[:, 4 * q : 4 * q + 4, :].rearrange("a r w -> r a w"),
-            )
+        nc.vector.memset(tab_s[:].rearrange("p a c -> p (a c)").bitcast(I32), 0)
+        nc.gpsimd.memset(w1_s[:].rearrange("p a c -> p (a c)").bitcast(I32), 0)
+
+        def load_scales(queue, plane, rows):
+            for q in (0, 2, 1, 3):
+                queue.dma_start(
+                    out=plane[QUAD * q : QUAD * q + 4, :, :].bitcast(I32),
+                    in_=rows.bitcast(I32)[:, 4 * q : 4 * q + 4, :].rearrange("a r w -> r a w"),
+                )
+
+        load_scales(nc.scalar, tab_s, tab_scales)
 
         def load_tab(a):
             nc.sync.dma_start(out=tab_w[a][:], in_=tab_words[a].rearrange("p t i -> p (t i)").bitcast(I32))
@@ -95,7 +90,7 @@ def tile_list_foam_slice_firmness_kernel(
         def load_w1(g):
             half = GROUP // 2
             nc.sync.dma_start(
-                out=w1_raw[g][:].bitcast(I32),
+                out=w1_w[g][:].bitcast(I32),
                 in_=w1_words.bitcast(I32)[:, :, g * half : (g + 1) * half].rearrange("a p w -> p a w"),
             )
 
@@ -118,65 +113,82 @@ def tile_list_foam_slice_firmness_kernel(
         def load_bulk(g):
             nc.sync.dma_start(out=firm[g][:], in_=dealt(bulk, g))
 
+        for tile, source in ((list1, offs), (list2, offs2), (list3, offs3), (list4, offs4)):
+            nc.sync.dma_start(tile[:], source)
+        nc.sync.dma_start(out=dn_t[:], in_=dn.rearrange("(g p t) -> p g t", g=GROUPS, t=PACK))
+        nc.sync.dma_start(out=up_t[:], in_=up.rearrange("(g p t) -> p g t", g=GROUPS, t=PACK))
         load_tab(0)
-        nc.sync.dma_start(list1[:], offs)
-        load_tab(1)
         load_w1(0)
+        load_tab(1)
+        load_scales(nc.sync, w1_s, w1_scales)
         load_tab(2)
         load_texture(0)
         load_gain(0, 1)
         load_page(0)
-        nc.sync.dma_start(list2[:], offs2)
-        nc.sync.dma_start(list3[:], offs3)
         load_texture(1)
-        load_gain(1, 2)
         load_w1(1)
-        nc.sync.dma_start(out=dn_t[:], in_=dn.rearrange("(g p t) -> p g t", g=GROUPS, t=PACK))
         load_page(1)
-        nc.sync.dma_start(out=up_t[:], in_=up.rearrange("(g p t) -> p g t", g=GROUPS, t=PACK))
-        load_gain(2, 4)
-        nc.sync.dma_start(list4[:], offs4)
+        load_gain(1, 4)
+        load_texture(2)
         chunks = [(b, g) for g in range(GROUPS) for b in range(GROUPS)]
         for s in range(2, SLICES):
-            load_texture(s)
+            if s + 1 < SLICES:
+                load_texture(s + 1)
             load_page(s)
             if s - 2 < len(chunks):
                 load_w2(*chunks[s - 2])
             else:
                 load_bulk(s - 2 - len(chunks))
 
-        picked_s = keep.tile([P, S], U8, name="picked_s", align_bytes=64)
-        nc.vector.tensor_copy(out=picked_s[:], in_=tab_s[:].indirect(list1[:]))
         for a in range(PASSES):
-            first = SPARE + 4 * a
-            nc.gpsimd.dma_start(
-                out=v_s[a][0:SHIFT_ROWS, :].bitcast(I32), in_=picked_s[first : first + SHIFT_ROWS, :].bitcast(I32)
-            )
-        for g in range(GROUPS):
-            nc.vector.tensor_copy(
-                out=w1_s[g][:],
-                in_=w1_sraw[:, :, g * GROUP : (g + 1) * GROUP].rearrange("p a (m t) -> p t a m", t=PACK),
-            )
-        for a in range(PASSES):
+            nc.vector.tensor_copy(out=v_s[a][:], in_=tab_s[:, a, :].indirect(list1[:]))
+        v_w = [
+            keep.tile([P, S], U32, name=f"v_w{a}", align_bytes=64)
+            for a in range(PASSES)
+        ]
+        for a in range(PASSES - 1):
             nc.vector.tensor_copy(out=v_w[a][:], in_=tab_w[a][:].bitcast(U32).indirect(list1[:]))
+        for c in range(BLOCKS):
+            nc.vector.tensor_copy(
+                out=v_w[PASSES - 1][:, c * P : (c + 1) * P],
+                in_=tab_w[PASSES - 1][:].bitcast(U32).indirect(list1[:, c * P // 16 : (c + 1) * P // 16]),
+            )
+        make_identity(nc, ident[:])
 
         for g in range(GROUPS):
-            nc.scalar.copy(out=w1_w[g][:], in_=w1_raw[g][:].rearrange("p a (m t) -> p t a m", t=PACK))
-            for t in range(PACK):
-                s = g * PACK + t
-                acc = psum.tile([P, S], F32, name=f"acc{s}", tag=f"bank{s}")
-                for a in range(PASSES):
+            accs = [psum.tile([P, GROUP], F32, name=f"acc{g}{c}", tag=f"bank{c}") for c in range(BLOCKS)]
+            for a in range(PASSES):
+                for c in range(BLOCKS):
                     nc.tensor.matmul_mx(
-                        out=acc[:],
-                        lhsT=w1_w[g][:, t, a, :].bitcast(FP4X4),
-                        lhsT_scale=w1_s[g][:, t, a, :],
-                        rhs=v_w[a][:].bitcast(FP8X4),
-                        rhs_scale=v_s[a][:],
+                        out=accs[c][:],
+                        lhsT=v_w[a][:, c * P : (c + 1) * P].bitcast(FP8X4),
+                        lhsT_scale=v_s[a][:, c * P : (c + 1) * P],
+                        rhs=w1_w[g][:, a, :].bitcast(FP4X4),
+                        rhs_scale=w1_s[:, a, g * GROUP : (g + 1) * GROUP],
                         start=(a == 0),
                         stop=(a == PASSES - 1),
                     )
-                nc.scalar.activation(out=entry[s][:], in_=acc[:], func=ACT.Tanh)
+            for ts in ([slice(0, 1), slice(1, PACK)] if g == 0 else [slice(0, PACK)]):
+                for c in range(BLOCKS):
+                    nc.scalar.activation(
+                        out=bent[g][:, c, ts, :],
+                        in_=accs[c][:].rearrange("p (m t) -> p t m", t=PACK)[:, ts, :],
+                        func=ACT.Tanh,
+                    )
 
+        def make_entries(s):
+            g, t = divmod(s, PACK)
+            turned = psum.tile([P, S], F32, name=f"turned{s}", tag=f"bank{BLOCKS + s % PACK}")
+            for c in range(BLOCKS):
+                nc.tensor.transpose(turned[:, c * P : (c + 1) * P], bent[g][:, c, t, :], ident[:])
+            if s == SLICES - 1:
+                entry = keep.tile([P, S], F32, name="entry_last", tag="last", align_bytes=64)
+            else:
+                entry = pair.tile([P, S], F32, name="entry")
+            nc.vector.tensor_tensor(out=entry[:], in0=turned[:], in1=tex[g][:, t, :], op=MULT)
+            return entry
+
+        entries = {0: make_entries(0)}
         for s in range(SLICES):
             g, t = divmod(s, PACK)
             if 0 <= s - 3 < len(chunks):
@@ -185,10 +197,9 @@ def tile_list_foam_slice_firmness_kernel(
                     out=w2_b[b2][g2][:].rearrange("p (t m i) -> p m i t", t=PACK, i=PACK),
                     in_=w2_raw[b2][g2][:].rearrange("p i (m t) -> p m i t", t=PACK),
                 )
-            nc.gpsimd.tensor_tensor(out=tex[g][:, t, :], in0=tex[g][:, t, :], in1=gain[:, t, :], op=MULT)
-            engine = nc.vector if s == 0 else nc.gpsimd
-            engine.tensor_tensor(out=entry[s][:], in0=entry[s][:], in1=tex[g][:, t, :], op=MULT)
-            nc.vector.tensor_copy(out=page[s][:].indirect(list2[:]), in_=entry[s][:])
+            nc.vector.tensor_tensor(out=page[s][:].indirect(list2[:]), in0=entries[s][:], in1=gain[:, t, :], op=MULT)
+            if s + 1 < SLICES:
+                entries[s + 1] = make_entries(s + 1)
             reread = ring.tile([P, PICK], F32, name="reread")
             nc.vector.tensor_copy(out=reread[:], in_=page[s][:].indirect(list3[:]))
             nc.scalar.activation(out=reread[:], in_=reread[:], func=ACT.Silu, scale=dn_t[:, g, t : t + 1])
@@ -198,7 +209,7 @@ def tile_list_foam_slice_firmness_kernel(
                     out=x_w[g][:].bitcast(FP8X4), scales=x_s[g][:], in_=x_b[g][:].rearrange("p j t -> p (j t)")
                 )
 
-        w2_s = keep.tile([P, GROUPS, H], U8, name="w2_s", tag=f"entry{SLICES - 1}", align_bytes=64)
+        w2_s = keep.tile([P, GROUPS, H], U8, name="w2_s", tag="last", align_bytes=64)
         for b, g in chunks:
             cols = slice(g * GROUP, (g + 1) * GROUP)
             nc.vector.quantize_mx(out=w2_w[:, b, cols].bitcast(FP8X4), scales=w2_s[:, b, cols], in_=w2_b[b][g][:])
@@ -209,9 +220,7 @@ def tile_list_foam_slice_firmness_kernel(
                 s = g * PACK + t
                 cols = slice(s * P, (s + 1) * P)
                 scale = dn_t[:, g, t : t + 1]
-                nc.gpsimd.tensor_scalar(
-                    out=firm[g][:, t, :], in0=firm[g][:, t, :], scalar1=scale, scalar2=0.0, op0=MULT, op1=ADD
-                )
+                nc.scalar.activation(out=firm[g][:, t, :], in_=firm[g][:, t, :], func=ACT.Copy, scale=scale)
                 acc = psum.tile([P, PICK], F32, name=f"sum{s}", tag=f"bank{s}")
                 for b in range(GROUPS):
                     nc.tensor.matmul_mx(
@@ -228,13 +237,15 @@ def tile_list_foam_slice_firmness_kernel(
                 )
                 nc.vector.tensor_tensor(out=y[:, t, :], in0=page[s][:].indirect(list4[:]), in1=firm[g][:, t, :], op=MULT)
                 nc.sync.dma_start(out=dealt(out_0, g)[:, t, :], in_=y[:, t, :])
-            rounded = y_b[g][:].rearrange("p (c i t) -> p c t i", i=4, t=PACK)
+            y_b = keep.tile([P, PICK * PACK], BF16, name=f"y_b{g}", tag=f"rounded0{g}", align_bytes=64)
+            rounded = y_b[:].rearrange("p (c i t) -> p c t i", i=4, t=PACK)
             exact = y[:].rearrange("p t (c i) -> p c t i", i=4)
             if g == 0:
                 nc.scalar.copy(out=rounded, in_=exact)
             else:
-                nc.vector.tensor_copy(out=rounded, in_=exact)
-            nc.vector.quantize_mx(out=y_w[g][:].bitcast(FP8X4), scales=y_s[g][:], in_=y_b[g][:])
+                nc.vector.tensor_copy(out=rounded[:, :VECTOR_RUNS], in_=exact[:, :VECTOR_RUNS])
+                nc.scalar.copy(out=rounded[:, VECTOR_RUNS:], in_=exact[:, VECTOR_RUNS:])
+            nc.vector.quantize_mx(out=y_w[g][:].bitcast(FP8X4), scales=y_s[g][:], in_=y_b[:])
             nc.sync.dma_start(out=out_1[g].rearrange("p m t -> p (m t)").bitcast(I32), in_=y_w[g][:].bitcast(I32))
             for q in range(QUADS):
                 queue = nc.scalar if q % 2 else nc.sync

@@ -25,7 +25,7 @@ PASSES = K // GROUP
 GROUPS = H // GROUP
 SLICES = GROUPS * PACK
 BLOCKS = S // P
-VECTOR_RUNS = 80
+RUN = 4
 QUADS = 4
 QUAD = P // QUADS
 
@@ -42,7 +42,6 @@ def tile_list_foam_slice_firmness_kernel(
     with ExitStack() as ctx:
         keep = ctx.enter_context(tc.tile_pool(name="keep", bufs=1))
         ring = ctx.enter_context(tc.tile_pool(name="ring", bufs=SLICES))
-        pair = ctx.enter_context(tc.tile_pool(name="pair", bufs=1))
         psum = ctx.enter_context(tc.psum_pool(name="psum", bufs=1))
 
         list1 = keep.tile([P, S // 16], U16, name="list1")
@@ -50,12 +49,13 @@ def tile_list_foam_slice_firmness_kernel(
         list3 = keep.tile([P, PICK // 16], U16, name="list3")
         list4 = keep.tile([P, PICK // 16], U16, name="list4")
 
-        tab_w = [keep.tile([P, T], I32, name=f"tab_w{a}", align_bytes=64) for a in range(PASSES)]
+        tab_w = [keep.tile([P, T], I32, name=f"tab_w{a}", tag=f"table{a}", align_bytes=64) for a in range(PASSES)]
         tab_s = keep.tile([P, PASSES, T], U8, name="tab_s", align_bytes=64)
         v_s = [keep.tile([P, S], U8, name=f"v_s{a}", align_bytes=64) for a in range(PASSES)]
-        w1_w = [keep.tile([P, PASSES, GROUP], U16, name=f"w1_w{g}", align_bytes=64) for g in range(GROUPS)]
-        w1_s = keep.tile([P, PASSES, H], U8, name="w1_s", align_bytes=64)
-        bent = [keep.tile([P, BLOCKS, PACK, P], F32, name=f"bent{g}") for g in range(GROUPS)]
+        w1_raw = [keep.tile([P, PASSES, GROUP], U16, name=f"w1_raw{g}", align_bytes=64) for g in range(GROUPS)]
+        w1_w = [keep.tile([P, PACK, PASSES, P], U16, name=f"w1_w{g}", align_bytes=64) for g in range(GROUPS)]
+        w1_sraw = keep.tile([P, PASSES, H], U8, name="w1_sraw", align_bytes=64)
+        x_rows = keep.tile([P, PACK, PICK], BF16, name="x_rows", align_bytes=64)
         ident = keep.tile([P, P], F32, name="ident")
         tex = [keep.tile([P, PACK, S], F32, name=f"tex{g}", tag=f"rows{g}") for g in range(GROUPS)]
         gain = keep.tile([P, PACK, S], F32, name="gain")
@@ -73,7 +73,7 @@ def tile_list_foam_slice_firmness_kernel(
         y_s = [keep.tile([P, PICK], U8, name=f"y_s{g}", align_bytes=64) for g in range(GROUPS)]
 
         nc.vector.memset(tab_s[:].rearrange("p a c -> p (a c)").bitcast(I32), 0)
-        nc.gpsimd.memset(w1_s[:].rearrange("p a c -> p (a c)").bitcast(I32), 0)
+        nc.gpsimd.memset(w1_sraw[:].rearrange("p a c -> p (a c)").bitcast(I32), 0)
 
         def load_scales(queue, plane, rows):
             for q in (0, 2, 1, 3):
@@ -90,7 +90,7 @@ def tile_list_foam_slice_firmness_kernel(
         def load_w1(g):
             half = GROUP // 2
             nc.sync.dma_start(
-                out=w1_w[g][:].bitcast(I32),
+                out=w1_raw[g][:].bitcast(I32),
                 in_=w1_words.bitcast(I32)[:, :, g * half : (g + 1) * half].rearrange("a p w -> p a w"),
             )
 
@@ -98,9 +98,9 @@ def tile_list_foam_slice_firmness_kernel(
             g, t = divmod(s, PACK)
             nc.sync.dma_start(out=tex[g][:, t, :], in_=dealt(texture, g)[:, t, :])
 
-        def load_gain(t0, t1):
+        def load_gain(t0, t1, quads=(0, 2, 1, 3)):
             rows = wgs.rearrange("(m t) j -> m t j", t=PACK)[:, t0:t1, :]
-            for q in (0, 2, 1, 3):
+            for q in quads:
                 nc.sync.dma_start(out=gain[QUAD * q : QUAD * (q + 1), t0:t1, :], in_=rows)
 
         def load_page(s):
@@ -115,21 +115,23 @@ def tile_list_foam_slice_firmness_kernel(
 
         for tile, source in ((list1, offs), (list2, offs2), (list3, offs3), (list4, offs4)):
             nc.sync.dma_start(tile[:], source)
-        nc.sync.dma_start(out=dn_t[:], in_=dn.rearrange("(g p t) -> p g t", g=GROUPS, t=PACK))
-        nc.sync.dma_start(out=up_t[:], in_=up.rearrange("(g p t) -> p g t", g=GROUPS, t=PACK))
+        load_gain(0, 1, (0, 2))
         load_tab(0)
         load_w1(0)
         load_tab(1)
-        load_scales(nc.sync, w1_s, w1_scales)
+        load_scales(nc.sync, w1_sraw, w1_scales)
         load_tab(2)
         load_texture(0)
-        load_gain(0, 1)
+        load_gain(0, 1, (1, 3))
         load_page(0)
         load_texture(1)
-        load_w1(1)
+        load_gain(1, 2)
+        nc.sync.dma_start(out=dn_t[:], in_=dn.rearrange("(g p t) -> p g t", g=GROUPS, t=PACK))
         load_page(1)
-        load_gain(1, 4)
+        nc.sync.dma_start(out=up_t[:], in_=up.rearrange("(g p t) -> p g t", g=GROUPS, t=PACK))
+        load_w1(1)
         load_texture(2)
+        load_gain(2, 4)
         chunks = [(b, g) for g in range(GROUPS) for b in range(GROUPS)]
         for s in range(2, SLICES):
             if s + 1 < SLICES:
@@ -137,115 +139,167 @@ def tile_list_foam_slice_firmness_kernel(
             load_page(s)
             if s - 2 < len(chunks):
                 load_w2(*chunks[s - 2])
-            else:
-                load_bulk(s - 2 - len(chunks))
+            if s == SLICES - 3:
+                load_bulk(1)
+                load_bulk(0)
 
+        v_w = [keep.tile([P, S], U32, name=f"v_w{a}", align_bytes=64) for a in range(PASSES)]
         for a in range(PASSES):
             nc.vector.tensor_copy(out=v_s[a][:], in_=tab_s[:, a, :].indirect(list1[:]))
-        v_w = [
-            keep.tile([P, S], U32, name=f"v_w{a}", align_bytes=64)
-            for a in range(PASSES)
-        ]
-        for a in range(PASSES - 1):
             nc.vector.tensor_copy(out=v_w[a][:], in_=tab_w[a][:].bitcast(U32).indirect(list1[:]))
-        for c in range(BLOCKS):
-            nc.vector.tensor_copy(
-                out=v_w[PASSES - 1][:, c * P : (c + 1) * P],
-                in_=tab_w[PASSES - 1][:].bitcast(U32).indirect(list1[:, c * P // 16 : (c + 1) * P // 16]),
-            )
         make_identity(nc, ident[:])
 
-        for g in range(GROUPS):
-            accs = [psum.tile([P, GROUP], F32, name=f"acc{g}{c}", tag=f"bank{c}") for c in range(BLOCKS)]
-            for a in range(PASSES):
-                for c in range(BLOCKS):
+        w1_cols = w1_sraw[:].rearrange("p a (g m t) -> p g t a m", g=GROUPS, t=PACK)
+        entries = []
+
+        def first_stage(g):
+            w1_s = keep.tile([P, PACK, PASSES, P], U8, name=f"w1_s{g}", tag="entry0" if g else "w1_s0", align_bytes=64)
+            for ts in ([slice(0, 1), slice(1, PACK)] if g == 0 else [slice(0, PACK)]):
+                nc.gpsimd.tensor_copy(out=w1_s[:, ts], in_=w1_cols[:, g, ts])
+            nc.scalar.copy(out=w1_w[g][:], in_=w1_raw[g][:].rearrange("p a (m t) -> p t a m", t=PACK))
+            for t in range(PACK):
+                s = g * PACK + t
+                acc = psum.tile([P, S], F32, name=f"acc{s}", tag=f"bank{s}")
+                for a in range(PASSES):
                     nc.tensor.matmul_mx(
-                        out=accs[c][:],
-                        lhsT=v_w[a][:, c * P : (c + 1) * P].bitcast(FP8X4),
-                        lhsT_scale=v_s[a][:, c * P : (c + 1) * P],
-                        rhs=w1_w[g][:, a, :].bitcast(FP4X4),
-                        rhs_scale=w1_s[:, a, g * GROUP : (g + 1) * GROUP],
+                        out=acc[:],
+                        lhsT=w1_w[g][:, t, a, :].bitcast(FP4X4),
+                        lhsT_scale=w1_s[:, t, a, :],
+                        rhs=v_w[a][:].bitcast(FP8X4),
+                        rhs_scale=v_s[a][:],
                         start=(a == 0),
                         stop=(a == PASSES - 1),
                     )
-            for ts in ([slice(0, 1), slice(1, PACK)] if g == 0 else [slice(0, PACK)]):
-                for c in range(BLOCKS):
-                    nc.scalar.activation(
-                        out=bent[g][:, c, ts, :],
-                        in_=accs[c][:].rearrange("p (m t) -> p t m", t=PACK)[:, ts, :],
-                        func=ACT.Tanh,
-                    )
+                entry = keep.tile([P, S], F32, name=f"entry{s}", tag="last" if s == SLICES - 1 else f"entry{s}", align_bytes=64)
+                nc.scalar.activation(out=entry[:], in_=acc[:], func=ACT.Tanh)
+                entries.append(entry)
 
-        def make_entries(s):
-            g, t = divmod(s, PACK)
-            turned = psum.tile([P, S], F32, name=f"turned{s}", tag=f"bank{BLOCKS + s % PACK}")
-            for c in range(BLOCKS):
-                nc.tensor.transpose(turned[:, c * P : (c + 1) * P], bent[g][:, c, t, :], ident[:])
-            if s == SLICES - 1:
-                entry = keep.tile([P, S], F32, name="entry_last", tag="last", align_bytes=64)
+        first_stage(0)
+
+        def round_w2(b, g):
+            if g == 0:
+                nc.scalar.copy(
+                    out=w2_b[b][g][:].rearrange("p (t m i) -> p m i t", t=PACK, i=PACK),
+                    in_=w2_raw[b][g][:].rearrange("p i (m t) -> p m i t", t=PACK),
+                )
             else:
-                entry = pair.tile([P, S], F32, name="entry")
-            nc.vector.tensor_tensor(out=entry[:], in0=turned[:], in1=tex[g][:, t, :], op=MULT)
-            return entry
+                nc.scalar.copy(
+                    out=w2_b[b][g][:].rearrange("p (c n i) -> p c i n", n=RUN, i=PACK),
+                    in_=w2_raw[b][g][:].rearrange("p i (c n) -> p c i n", n=RUN),
+                )
 
-        entries = {0: make_entries(0)}
+        bulk_t = keep.tile([P, BLOCKS, PACK, P], F32, name="bulk_t", tag="table0", align_bytes=64)
+
+        def prepare_bulk():
+            for t in range(PACK):
+                turned = psum.tile([P, BLOCKS, P], F32, name=f"bulk_turned{t}", tag=f"bank{t}")
+                for c in range(BLOCKS):
+                    nc.tensor.transpose(turned[:, c, :], firm[1][:, t, c * P : (c + 1) * P], ident[:])
+                nc.scalar.copy(out=bulk_t[:, :, t, :], in_=turned[:])
+            for t in range(PACK):
+                nc.gpsimd.tensor_scalar(
+                    out=firm[0][:, t, :], in0=firm[0][:, t, :], scalar1=dn_t[:, 0, t : t + 1], scalar2=0.0, op0=MULT, op1=ADD
+                )
+
+        def pieces(parts, width):
+            step = width // parts
+            return [(slice(i * step, (i + 1) * step), slice(i * step // 16, (i + 1) * step // 16)) for i in range(parts)]
+
         for s in range(SLICES):
             g, t = divmod(s, PACK)
-            if 0 <= s - 3 < len(chunks):
-                b2, g2 = chunks[s - 3]
-                nc.scalar.copy(
-                    out=w2_b[b2][g2][:].rearrange("p (t m i) -> p m i t", t=PACK, i=PACK),
-                    in_=w2_raw[b2][g2][:].rearrange("p i (m t) -> p m i t", t=PACK),
-                )
-            nc.vector.tensor_tensor(out=page[s][:].indirect(list2[:]), in0=entries[s][:], in1=gain[:, t, :], op=MULT)
-            if s + 1 < SLICES:
-                entries[s + 1] = make_entries(s + 1)
+            if s == 1:
+                first_stage(1)
+            if 0 <= s - 2 < len(chunks):
+                round_w2(*chunks[s - 2])
+            if s == SLICES - 2:
+                prepare_bulk()
+            nc.gpsimd.tensor_tensor(out=tex[g][:, t, :], in0=tex[g][:, t, :], in1=gain[:, t, :], op=MULT)
+            engine = nc.vector if s == 0 else nc.gpsimd
+            engine.tensor_tensor(out=entries[s][:], in0=entries[s][:], in1=tex[g][:, t, :], op=MULT)
+            nc.vector.tensor_copy(out=page[s][:].indirect(list2[:]), in_=entries[s][:])
             reread = ring.tile([P, PICK], F32, name="reread")
-            nc.vector.tensor_copy(out=reread[:], in_=page[s][:].indirect(list3[:]))
-            nc.scalar.activation(out=reread[:], in_=reread[:], func=ACT.Silu, scale=dn_t[:, g, t : t + 1])
-            nc.scalar.activation(out=x_b[g][:, :, t], in_=reread[:], func=ACT.Copy, scale=up_t[:, g, t : t + 1])
-            if t == PACK - 1:
-                nc.vector.quantize_mx(
-                    out=x_w[g][:].bitcast(FP8X4), scales=x_s[g][:], in_=x_b[g][:].rearrange("p j t -> p (j t)")
-                )
+            for cols, part in pieces(2 if s == SLICES - 1 else 1, PICK):
+                nc.vector.tensor_copy(out=reread[:, cols], in_=page[s][:].indirect(list3[:, part]))
+                nc.scalar.activation(out=reread[:, cols], in_=reread[:, cols], func=ACT.Silu, scale=dn_t[:, g, t : t + 1])
+                rounded = x_rows[:, t, cols] if g == 0 else x_b[g][:, cols, t]
+                nc.scalar.activation(out=rounded, in_=reread[:, cols], func=ACT.Copy, scale=up_t[:, g, t : t + 1])
+                if t == PACK - 1:
+                    if g == 0:
+                        nc.scalar.copy(
+                            out=x_b[g][:].rearrange("p (c n) t -> p c t n", n=RUN),
+                            in_=x_rows[:].rearrange("p t (c n) -> p c t n", n=RUN),
+                        )
+                    nc.vector.quantize_mx(
+                        out=x_w[g][:, cols].bitcast(FP8X4),
+                        scales=x_s[g][:, cols],
+                        in_=x_b[g][:, cols, :].rearrange("p j t -> p (j t)"),
+                    )
 
         w2_s = keep.tile([P, GROUPS, H], U8, name="w2_s", tag="last", align_bytes=64)
         for b, g in chunks:
             cols = slice(g * GROUP, (g + 1) * GROUP)
             nc.vector.quantize_mx(out=w2_w[:, b, cols].bitcast(FP8X4), scales=w2_s[:, b, cols], in_=w2_b[b][g][:])
 
+        def product(acc, stationary, moving):
+            for b in range(GROUPS):
+                (l_w, l_s), (r_w, r_s) = stationary(b), moving(b)
+                nc.tensor.matmul_mx(
+                    out=acc[:],
+                    lhsT=l_w.bitcast(FP8X4),
+                    lhsT_scale=l_s,
+                    rhs=r_w.bitcast(FP8X4),
+                    rhs_scale=r_s,
+                    start=(b == 0),
+                    stop=(b == GROUPS - 1),
+                )
+
+        direct = []
+        for t in range(PACK):
+            acc = psum.tile([P, PICK], F32, name=f"sum{t}", tag=f"bank{t}")
+            cols = slice(t * P, (t + 1) * P)
+            product(acc, lambda b: (w2_w[:, b, cols], w2_s[:, b, cols]), lambda b: (x_w[b][:], x_s[b][:]))
+            direct.append(acc)
+        sums_t = keep.tile([P, BLOCKS, PACK, P], F32, name="sums_t", tag="table1", align_bytes=64)
+        for c in range(BLOCKS):
+            acc = psum.tile([P, GROUP], F32, name=f"sum_t{c}", tag=f"bank{BLOCKS + c}")
+            cols = slice(c * P, (c + 1) * P)
+            product(acc, lambda b: (x_w[b][:, cols], x_s[b][:, cols]), lambda b: (w2_w[:, b, GROUP:], w2_s[:, b, GROUP:]))
+            nc.scalar.copy(out=sums_t[:, c, :, :], in_=acc[:].rearrange("p (m t) -> p t m", t=PACK))
+
         for g in range(GROUPS):
             y = keep.tile([P, PACK, PICK], F32, name=f"y{g}", tag=f"rows{g}")
+            y_b = keep.tile([P, PICK, PACK], BF16, name=f"y_b{g}", tag="table1" if g == 0 else "rounded01", align_bytes=64)
             for t in range(PACK):
                 s = g * PACK + t
-                cols = slice(s * P, (s + 1) * P)
                 scale = dn_t[:, g, t : t + 1]
-                nc.scalar.activation(out=firm[g][:, t, :], in_=firm[g][:, t, :], func=ACT.Copy, scale=scale)
-                acc = psum.tile([P, PICK], F32, name=f"sum{s}", tag=f"bank{s}")
-                for b in range(GROUPS):
-                    nc.tensor.matmul_mx(
-                        out=acc[:],
-                        lhsT=w2_w[:, b, cols].bitcast(FP8X4),
-                        lhsT_scale=w2_s[:, b, cols],
-                        rhs=x_w[b][:].bitcast(FP8X4),
-                        rhs_scale=x_s[b][:],
-                        start=(b == 0),
-                        stop=(b == GROUPS - 1),
+                if g == 0:
+                    nc.vector.scalar_tensor_tensor(
+                        out=firm[g][:, t, :], in0=direct[t][:], scalar=scale, in1=firm[g][:, t, :], op0=MULT, op1=ADD
                     )
-                nc.vector.scalar_tensor_tensor(
-                    out=firm[g][:, t, :], in0=acc[:], scalar=scale, in1=firm[g][:, t, :], op0=MULT, op1=ADD
-                )
-                nc.vector.tensor_tensor(out=y[:, t, :], in0=page[s][:].indirect(list4[:]), in1=firm[g][:, t, :], op=MULT)
-                nc.sync.dma_start(out=dealt(out_0, g)[:, t, :], in_=y[:, t, :])
-            y_b = keep.tile([P, PICK * PACK], BF16, name=f"y_b{g}", tag=f"rounded0{g}", align_bytes=64)
-            rounded = y_b[:].rearrange("p (c i t) -> p c t i", i=4, t=PACK)
-            exact = y[:].rearrange("p t (c i) -> p c t i", i=4)
-            if g == 0:
-                nc.scalar.copy(out=rounded, in_=exact)
-            else:
-                nc.vector.tensor_copy(out=rounded[:, :VECTOR_RUNS], in_=exact[:, :VECTOR_RUNS])
-                nc.scalar.copy(out=rounded[:, VECTOR_RUNS:], in_=exact[:, VECTOR_RUNS:])
-            nc.vector.quantize_mx(out=y_w[g][:].bitcast(FP8X4), scales=y_s[g][:], in_=y_b[:])
+                else:
+                    back = psum.tile([P, BLOCKS, P], F32, name=f"back{t}", tag=f"bank{t}")
+                    for c in range(BLOCKS):
+                        for term, first in ((bulk_t, True), (sums_t, False)):
+                            nc.tensor.matmul(
+                                back[:, c, :], term[:, c, t, :], ident[:], start=first, stop=not first, is_transpose=True
+                            )
+                    nc.scalar.activation(
+                        out=firm[g][:, t, :], in_=back[:].rearrange("p c j -> p (c j)"), func=ACT.Copy, scale=scale
+                    )
+                halves = pieces(2 if s == SLICES - 1 else 1, PICK)
+                for i, (cols, part) in enumerate(halves):
+                    nc.vector.tensor_tensor(
+                        out=y[:, t, cols], in0=page[s][:].indirect(list4[:, part]), in1=firm[g][:, t, cols], op=MULT
+                    )
+                    nc.sync.dma_start(out=dealt(out_0, g)[:, t, cols], in_=y[:, t, cols])
+                    if t == PACK - 1:
+                        rounded = y_b[:, cols, :].rearrange("p (c n) t -> p c t n", n=RUN)
+                        exact = y[:, :, cols].rearrange("p t (c n) -> p c t n", n=RUN)
+                        if i == 0:
+                            nc.scalar.copy(out=rounded, in_=exact)
+                        else:
+                            nc.vector.tensor_copy(out=rounded, in_=exact)
+            nc.vector.quantize_mx(out=y_w[g][:].bitcast(FP8X4), scales=y_s[g][:], in_=y_b[:].rearrange("p j t -> p (j t)"))
             nc.sync.dma_start(out=out_1[g].rearrange("p m t -> p (m t)").bitcast(I32), in_=y_w[g][:].bitcast(I32))
             for q in range(QUADS):
                 queue = nc.scalar if q % 2 else nc.sync

@@ -54,7 +54,7 @@ def tile_list_foam_slice_firmness_kernel(
         v_s = [keep.tile([P, S], U8, name=f"v_s{a}", align_bytes=64) for a in range(PASSES)]
         w1_raw = [keep.tile([P, PASSES, GROUP], U16, name=f"w1_raw{g}", align_bytes=64) for g in range(GROUPS)]
         w1_w = [keep.tile([P, PACK, PASSES, P], U16, name=f"w1_w{g}", align_bytes=64) for g in range(GROUPS)]
-        w1_sraw = keep.tile([P, PASSES, H], U8, name="w1_sraw", align_bytes=64)
+        w1_sraw = [keep.tile([P, PASSES, GROUP], U8, name=f"w1_sraw{g}", align_bytes=64) for g in range(GROUPS)]
         x_rows = keep.tile([P, PACK, PICK], BF16, name="x_rows", align_bytes=64)
         ident = keep.tile([P, P], F32, name="ident")
         tex = [keep.tile([P, PACK, S], F32, name=f"tex{g}", tag=f"rows{g}") for g in range(GROUPS)]
@@ -67,22 +67,23 @@ def tile_list_foam_slice_firmness_kernel(
         w2_w = keep.tile([P, GROUPS, H], U32, name="w2_w", align_bytes=64)
         x_b = [keep.tile([P, PICK, PACK], BF16, name=f"x_b{b}", align_bytes=64) for b in range(GROUPS)]
         x_w = [keep.tile([P, PICK], U32, name=f"x_w{b}", align_bytes=64) for b in range(GROUPS)]
-        x_s = [keep.tile([P, PICK], U8, name=f"x_s{b}", align_bytes=64) for b in range(GROUPS)]
+        x_s1 = keep.tile([P, PICK], U8, name="x_s1", align_bytes=64)
         firm = [keep.tile([P, PACK, PICK], F32, name=f"firm{g}") for g in range(GROUPS)]
         y_w = [keep.tile([P, PICK], U32, name=f"y_w{g}", align_bytes=64) for g in range(GROUPS)]
         y_s = [keep.tile([P, PICK], U8, name=f"y_s{g}", align_bytes=64) for g in range(GROUPS)]
 
         nc.vector.memset(tab_s[:].rearrange("p a c -> p (a c)").bitcast(I32), 0)
-        nc.gpsimd.memset(w1_sraw[:].rearrange("p a c -> p (a c)").bitcast(I32), 0)
+        for g in range(GROUPS):
+            nc.gpsimd.memset(w1_sraw[g][:].rearrange("p a c -> p (a c)").bitcast(I32), 0)
 
         def load_scales(queue, plane, rows):
             for q in (0, 2, 1, 3):
                 queue.dma_start(
                     out=plane[QUAD * q : QUAD * q + 4, :, :].bitcast(I32),
-                    in_=rows.bitcast(I32)[:, 4 * q : 4 * q + 4, :].rearrange("a r w -> r a w"),
+                    in_=rows[:, 4 * q : 4 * q + 4, :].rearrange("a r w -> r a w"),
                 )
 
-        load_scales(nc.scalar, tab_s, tab_scales)
+        load_scales(nc.scalar, tab_s, tab_scales.bitcast(I32))
 
         def load_tab(a):
             nc.sync.dma_start(out=tab_w[a][:], in_=tab_words[a].rearrange("p t i -> p (t i)").bitcast(I32))
@@ -119,17 +120,18 @@ def tile_list_foam_slice_firmness_kernel(
         load_tab(0)
         load_w1(0)
         load_tab(1)
-        load_scales(nc.sync, w1_sraw, w1_scales)
+        load_scales(nc.sync, w1_sraw[0], w1_scales.bitcast(I32)[:, :, : GROUP // 4])
         load_tab(2)
         load_texture(0)
         load_gain(0, 1, (1, 3))
         load_page(0)
+        load_w1(1)
+        load_scales(nc.sync, w1_sraw[1], w1_scales.bitcast(I32)[:, :, GROUP // 4 :])
         load_texture(1)
         load_gain(1, 2)
         nc.sync.dma_start(out=dn_t[:], in_=dn.rearrange("(g p t) -> p g t", g=GROUPS, t=PACK))
         load_page(1)
         nc.sync.dma_start(out=up_t[:], in_=up.rearrange("(g p t) -> p g t", g=GROUPS, t=PACK))
-        load_w1(1)
         load_texture(2)
         load_gain(2, 4)
         chunks = [(b, g) for g in range(GROUPS) for b in range(GROUPS)]
@@ -149,13 +151,12 @@ def tile_list_foam_slice_firmness_kernel(
             nc.vector.tensor_copy(out=v_w[a][:], in_=tab_w[a][:].bitcast(U32).indirect(list1[:]))
         make_identity(nc, ident[:])
 
-        w1_cols = w1_sraw[:].rearrange("p a (g m t) -> p g t a m", g=GROUPS, t=PACK)
         entries = []
 
         def first_stage(g):
-            w1_s = keep.tile([P, PACK, PASSES, P], U8, name=f"w1_s{g}", tag="entry0" if g else "w1_s0", align_bytes=64)
+            w1_s = keep.tile([P, PACK, PASSES, P], U8, name=f"w1_s{g}", align_bytes=64)
             for ts in ([slice(0, 1), slice(1, PACK)] if g == 0 else [slice(0, PACK)]):
-                nc.gpsimd.tensor_copy(out=w1_s[:, ts], in_=w1_cols[:, g, ts])
+                nc.gpsimd.tensor_copy(out=w1_s[:, ts], in_=w1_sraw[g][:].rearrange("p a (m t) -> p t a m", t=PACK)[:, ts])
             nc.scalar.copy(out=w1_w[g][:], in_=w1_raw[g][:].rearrange("p a (m t) -> p t a m", t=PACK))
             for t in range(PACK):
                 s = g * PACK + t
@@ -174,7 +175,8 @@ def tile_list_foam_slice_firmness_kernel(
                 nc.scalar.activation(out=entry[:], in_=acc[:], func=ACT.Tanh)
                 entries.append(entry)
 
-        first_stage(0)
+        for g in range(GROUPS):
+            first_stage(g)
 
         def round_w2(b, g):
             if g == 0:
@@ -207,14 +209,12 @@ def tile_list_foam_slice_firmness_kernel(
 
         for s in range(SLICES):
             g, t = divmod(s, PACK)
-            if s == 1:
-                first_stage(1)
             if 0 <= s - 2 < len(chunks):
                 round_w2(*chunks[s - 2])
             if s == SLICES - 2:
                 prepare_bulk()
-            nc.gpsimd.tensor_tensor(out=tex[g][:, t, :], in0=tex[g][:, t, :], in1=gain[:, t, :], op=MULT)
             engine = nc.vector if s == 0 else nc.gpsimd
+            engine.tensor_tensor(out=tex[g][:, t, :], in0=tex[g][:, t, :], in1=gain[:, t, :], op=MULT)
             engine.tensor_tensor(out=entries[s][:], in0=entries[s][:], in1=tex[g][:, t, :], op=MULT)
             nc.vector.tensor_copy(out=page[s][:].indirect(list2[:]), in_=entries[s][:])
             reread = ring.tile([P, PICK], F32, name="reread")
@@ -223,19 +223,22 @@ def tile_list_foam_slice_firmness_kernel(
                 nc.scalar.activation(out=reread[:, cols], in_=reread[:, cols], func=ACT.Silu, scale=dn_t[:, g, t : t + 1])
                 rounded = x_rows[:, t, cols] if g == 0 else x_b[g][:, cols, t]
                 nc.scalar.activation(out=rounded, in_=reread[:, cols], func=ACT.Copy, scale=up_t[:, g, t : t + 1])
-                if t == PACK - 1:
-                    if g == 0:
-                        nc.scalar.copy(
-                            out=x_b[g][:].rearrange("p (c n) t -> p c t n", n=RUN),
-                            in_=x_rows[:].rearrange("p t (c n) -> p c t n", n=RUN),
-                        )
+                if s == PACK - 1:
+                    nc.scalar.copy(
+                        out=x_b[g][:].rearrange("p (c n) t -> p c t n", n=RUN),
+                        in_=x_rows[:].rearrange("p t (c n) -> p c t n", n=RUN),
+                    )
+                if s == SLICES - 1:
                     nc.vector.quantize_mx(
                         out=x_w[g][:, cols].bitcast(FP8X4),
-                        scales=x_s[g][:, cols],
+                        scales=x_s1[:, cols],
                         in_=x_b[g][:, cols, :].rearrange("p j t -> p (j t)"),
                     )
 
-        w2_s = keep.tile([P, GROUPS, H], U8, name="w2_s", tag="last", align_bytes=64)
+        late_s = keep.tile([P, GROUPS * H + PICK], U8, name="late_s", tag="last", align_bytes=64)
+        w2_s = late_s[:, : GROUPS * H].rearrange("p (b n) -> p b n", b=GROUPS)
+        x_s = [late_s[:, GROUPS * H :], x_s1[:]]
+        nc.vector.quantize_mx(out=x_w[0][:].bitcast(FP8X4), scales=x_s[0], in_=x_b[0][:].rearrange("p j t -> p (j t)"))
         for b, g in chunks:
             cols = slice(g * GROUP, (g + 1) * GROUP)
             nc.vector.quantize_mx(out=w2_w[:, b, cols].bitcast(FP8X4), scales=w2_s[:, b, cols], in_=w2_b[b][g][:])
@@ -257,7 +260,7 @@ def tile_list_foam_slice_firmness_kernel(
         for t in range(PACK):
             acc = psum.tile([P, PICK], F32, name=f"sum{t}", tag=f"bank{t}")
             cols = slice(t * P, (t + 1) * P)
-            product(acc, lambda b: (w2_w[:, b, cols], w2_s[:, b, cols]), lambda b: (x_w[b][:], x_s[b][:]))
+            product(acc, lambda b: (w2_w[:, b, cols], w2_s[:, b, cols]), lambda b: (x_w[b][:], x_s[b]))
             direct.append(acc)
         sums_t = keep.tile([P, BLOCKS, PACK, P], F32, name="sums_t", tag="table1", align_bytes=64)
         for c in range(BLOCKS):

from contextlib import ExitStack

import concourse.mybir as mybir
from concourse.masks import make_identity

K, H, T, S, T2, PICK = 1536, 1024, 2048, 512, 1024, 512
FLOPS = 2 * K * H * S + 2 * H * H * PICK

F32 = mybir.dt.float32
BF16 = mybir.dt.bfloat16
I32 = mybir.dt.int32
U32 = mybir.dt.uint32
U16 = mybir.dt.uint16
U8 = mybir.dt.uint8
FP8X4 = mybir.dt.float8_e4m3fn_x4
FP4X4 = mybir.dt.float4_e2m1fn_x4
ACT = mybir.ActivationFunctionType
MULT = mybir.AluOpType.mult
ADD = mybir.AluOpType.add

P = 128
PACK = 4
GROUP = P * PACK
PASSES = K // GROUP
GROUPS = H // GROUP
SLICES = GROUPS * PACK
BLOCKS = S // P
RUN = 4
QUADS = 4
QUAD = P // QUADS


def tile_list_foam_slice_firmness_kernel(
    tc, tab_words, tab_scales, offs, w1_words, w1_scales, texture, page0, wgs, offs2, dn, offs3, up, w2, bulk, offs4,
    out_0, out_1, out_2,
):
    nc = tc.nc

    def dealt(rows, g):
        return rows[g * GROUP : (g + 1) * GROUP, :].rearrange("(p t) j -> p t j", t=PACK)

    with ExitStack() as ctx:
        keep = ctx.enter_context(tc.tile_pool(name="keep", bufs=1))
        ring = ctx.enter_context(tc.tile_pool(name="ring", bufs=SLICES))
        psum = ctx.enter_context(tc.psum_pool(name="psum", bufs=1))

        list1 = keep.tile([P, S // 16], U16, name="list1")
        list2 = keep.tile([P, S // 16], U16, name="list2")
        list3 = keep.tile([P, PICK // 16], U16, name="list3")
        list4 = keep.tile([P, PICK // 16], U16, name="list4")

        tab_w = [keep.tile([P, T], I32, name=f"tab_w{a}", tag=f"table{a}", align_bytes=64) for a in range(PASSES)]
        tab_s = keep.tile([P, PASSES, T], U8, name="tab_s", align_bytes=64)
        v_s = [keep.tile([P, S], U8, name=f"v_s{a}", align_bytes=64) for a in range(PASSES)]
        w1_raw = [keep.tile([P, PASSES, GROUP], U16, name=f"w1_raw{g}", align_bytes=64) for g in range(GROUPS)]
        w1_w = [keep.tile([P, PACK, PASSES, P], U16, name=f"w1_w{g}", align_bytes=64) for g in range(GROUPS)]
        w1_sraw = [keep.tile([P, PASSES, GROUP], U8, name=f"w1_sraw{g}", align_bytes=64) for g in range(GROUPS)]
        x_rows = keep.tile([P, PACK, PICK], BF16, name="x_rows", align_bytes=64)
        ident = keep.tile([P, P], F32, name="ident")
        tex = [keep.tile([P, PACK, S], F32, name=f"tex{g}", tag=f"rows{g}") for g in range(GROUPS)]
        gain = keep.tile([P, PACK, S], F32, name="gain")
        page = [keep.tile([P, T2], F32, name=f"page{s}") for s in range(SLICES)]
        dn_t = keep.tile([P, GROUPS, PACK], F32, name="dn_t")
        up_t = keep.tile([P, GROUPS, PACK], F32, name="up_t")
        w2_raw = [[keep.tile([P, PACK, GROUP], F32, name=f"w2_raw{b}{g}") for g in range(GROUPS)] for b in range(GROUPS)]
        w2_b = [[keep.tile([P, PACK * GROUP], BF16, name=f"w2_b{b}{g}", tag=f"rounded{b}{g}", align_bytes=64) for g in range(GROUPS)] for b in range(GROUPS)]
        w2_w = keep.tile([P, GROUPS, H], U32, name="w2_w", align_bytes=64)
        x_b = [keep.tile([P, PICK, PACK], BF16, name=f"x_b{b}", align_bytes=64) for b in range(GROUPS)]
        x_w = [keep.tile([P, PICK], U32, name=f"x_w{b}", align_bytes=64) for b in range(GROUPS)]
        x_s1 = keep.tile([P, PICK], U8, name="x_s1", align_bytes=64)
        firm = [keep.tile([P, PACK, PICK], F32, name=f"firm{g}") for g in range(GROUPS)]
        y_w = [keep.tile([P, PICK], U32, name=f"y_w{g}", align_bytes=64) for g in range(GROUPS)]
        y_s = [keep.tile([P, PICK], U8, name=f"y_s{g}", align_bytes=64) for g in range(GROUPS)]

        nc.vector.memset(tab_s[:].rearrange("p a c -> p (a c)").bitcast(I32), 0)
        for g in range(GROUPS):
            nc.gpsimd.memset(w1_sraw[g][:].rearrange("p a c -> p (a c)").bitcast(I32), 0)

        def load_scales(queue, plane, rows):
            for q in (0, 2, 1, 3):
                queue.dma_start(
                    out=plane[QUAD * q : QUAD * q + 4, :, :].bitcast(I32),
                    in_=rows[:, 4 * q : 4 * q + 4, :].rearrange("a r w -> r a w"),
                )

        load_scales(nc.scalar, tab_s, tab_scales.bitcast(I32))

        def load_tab(a):
            nc.sync.dma_start(out=tab_w[a][:], in_=tab_words[a].rearrange("p t i -> p (t i)").bitcast(I32))

        def load_w1(g):
            half = GROUP // 2
            nc.sync.dma_start(
                out=w1_raw[g][:].bitcast(I32),
                in_=w1_words.bitcast(I32)[:, :, g * half : (g + 1) * half].rearrange("a p w -> p a w"),
            )

        def load_texture(s):
            g, t = divmod(s, PACK)
            nc.sync.dma_start(out=tex[g][:, t, :], in_=dealt(texture, g)[:, t, :])

        def load_gain(t0, t1, quads=(0, 2, 1, 3)):
            rows = wgs.rearrange("(m t) j -> m t j", t=PACK)[:, t0:t1, :]
            for q in quads:
                nc.sync.dma_start(out=gain[QUAD * q : QUAD * (q + 1), t0:t1, :], in_=rows)

        def load_page(s):
            g, t = divmod(s, PACK)
            nc.sync.dma_start(out=page[s][:], in_=dealt(page0, g)[:, t, :])

        def load_w2(b, g):
            nc.sync.dma_start(out=w2_raw[b][g][:], in_=dealt(w2, b)[:, :, g * GROUP : (g + 1) * GROUP])

        def load_bulk(g):
            nc.sync.dma_start(out=firm[g][:], in_=dealt(bulk, g))

        for tile, source in ((list1, offs), (list2, offs2), (list3, offs3), (list4, offs4)):
            nc.sync.dma_start(tile[:], source)
        load_gain(0, 1, (0, 2))
        load_tab(0)
        load_w1(0)
        load_tab(1)
        load_scales(nc.sync, w1_sraw[0], w1_scales.bitcast(I32)[:, :, : GROUP // 4])
        load_tab(2)
        load_texture(0)
        load_gain(0, 1, (1, 3))
        load_page(0)
        load_w1(1)
        load_scales(nc.sync, w1_sraw[1], w1_scales.bitcast(I32)[:, :, GROUP // 4 :])
        load_texture(1)
        load_gain(1, 2)
        nc.sync.dma_start(out=dn_t[:], in_=dn.rearrange("(g p t) -> p g t", g=GROUPS, t=PACK))
        load_page(1)
        nc.sync.dma_start(out=up_t[:], in_=up.rearrange("(g p t) -> p g t", g=GROUPS, t=PACK))
        load_texture(2)
        load_gain(2, 4)
        chunks = [(b, g) for g in range(GROUPS) for b in range(GROUPS)]
        for s in range(2, SLICES):
            if s + 1 < SLICES:
                load_texture(s + 1)
            load_page(s)
            if s - 2 < len(chunks):
                load_w2(*chunks[s - 2])
            if s == SLICES - 3:
                load_bulk(1)
                load_bulk(0)

        v_w = [keep.tile([P, S], U32, name=f"v_w{a}", align_bytes=64) for a in range(PASSES)]
        for a in range(PASSES):
            nc.vector.tensor_copy(out=v_s[a][:], in_=tab_s[:, a, :].indirect(list1[:]))
            nc.vector.tensor_copy(out=v_w[a][:], in_=tab_w[a][:].bitcast(U32).indirect(list1[:]))
        make_identity(nc, ident[:])

        entries = []

        def first_stage(g):
            w1_s = keep.tile([P, PACK, PASSES, P], U8, name=f"w1_s{g}", align_bytes=64)
            for ts in ([slice(0, 1), slice(1, PACK)] if g == 0 else [slice(0, PACK)]):
                nc.gpsimd.tensor_copy(out=w1_s[:, ts], in_=w1_sraw[g][:].rearrange("p a (m t) -> p t a m", t=PACK)[:, ts])
            nc.scalar.copy(out=w1_w[g][:], in_=w1_raw[g][:].rearrange("p a (m t) -> p t a m", t=PACK))
            for t in range(PACK):
                s = g * PACK + t
                acc = psum.tile([P, S], F32, name=f"acc{s}", tag=f"bank{s}")
                for a in range(PASSES):
                    nc.tensor.matmul_mx(
                        out=acc[:],
                        lhsT=w1_w[g][:, t, a, :].bitcast(FP4X4),
                        lhsT_scale=w1_s[:, t, a, :],
                        rhs=v_w[a][:].bitcast(FP8X4),
                        rhs_scale=v_s[a][:],
                        start=(a == 0),
                        stop=(a == PASSES - 1),
                    )
                entry = keep.tile([P, S], F32, name=f"entry{s}", tag="last" if s == SLICES - 1 else f"entry{s}", align_bytes=64)
                nc.scalar.activation(out=entry[:], in_=acc[:], func=ACT.Tanh)
                entries.append(entry)

        for g in range(GROUPS):
            first_stage(g)

        def round_w2(b, g):
            if g == 0:
                nc.scalar.copy(
                    out=w2_b[b][g][:].rearrange("p (t m i) -> p m i t", t=PACK, i=PACK),
                    in_=w2_raw[b][g][:].rearrange("p i (m t) -> p m i t", t=PACK),
                )
            else:
                nc.scalar.copy(
                    out=w2_b[b][g][:].rearrange("p (c n i) -> p c i n", n=RUN, i=PACK),
                    in_=w2_raw[b][g][:].rearrange("p i (c n) -> p c i n", n=RUN),
                )

        bulk_t = keep.tile([P, BLOCKS, PACK, P], F32, name="bulk_t", tag="table0", align_bytes=64)

        def prepare_bulk():
            for t in range(PACK):
                turned = psum.tile([P, BLOCKS, P], F32, name=f"bulk_turned{t}", tag=f"bank{t}")
                for c in range(BLOCKS):
                    nc.tensor.transpose(turned[:, c, :], firm[1][:, t, c * P : (c + 1) * P], ident[:])
                nc.scalar.copy(out=bulk_t[:, :, t, :], in_=turned[:])
            for t in range(PACK):
                nc.gpsimd.tensor_scalar(
                    out=firm[0][:, t, :], in0=firm[0][:, t, :], scalar1=dn_t[:, 0, t : t + 1], scalar2=0.0, op0=MULT, op1=ADD
                )

        def pieces(parts, width):
            step = width // parts
            return [(slice(i * step, (i + 1) * step), slice(i * step // 16, (i + 1) * step // 16)) for i in range(parts)]

        for s in range(SLICES):
            g, t = divmod(s, PACK)
            if 0 <= s - 2 < len(chunks):
                round_w2(*chunks[s - 2])
            if s == SLICES - 2:
                prepare_bulk()
            engine = nc.vector if s == 0 else nc.gpsimd
            engine.tensor_tensor(out=tex[g][:, t, :], in0=tex[g][:, t, :], in1=gain[:, t, :], op=MULT)
            engine.tensor_tensor(out=entries[s][:], in0=entries[s][:], in1=tex[g][:, t, :], op=MULT)
            nc.vector.tensor_copy(out=page[s][:].indirect(list2[:]), in_=entries[s][:])
            reread = ring.tile([P, PICK], F32, name="reread")
            for cols, part in pieces(2 if s == SLICES - 1 else 1, PICK):
                nc.vector.tensor_copy(out=reread[:, cols], in_=page[s][:].indirect(list3[:, part]))
                nc.scalar.activation(out=reread[:, cols], in_=reread[:, cols], func=ACT.Silu, scale=dn_t[:, g, t : t + 1])
                rounded = x_rows[:, t, cols] if g == 0 else x_b[g][:, cols, t]
                nc.scalar.activation(out=rounded, in_=reread[:, cols], func=ACT.Copy, scale=up_t[:, g, t : t + 1])
                if s == PACK - 1:
                    nc.scalar.copy(
                        out=x_b[g][:].rearrange("p (c n) t -> p c t n", n=RUN),
                        in_=x_rows[:].rearrange("p t (c n) -> p c t n", n=RUN),
                    )
                if s == SLICES - 1:
                    nc.vector.quantize_mx(
                        out=x_w[g][:, cols].bitcast(FP8X4),
                        scales=x_s1[:, cols],
                        in_=x_b[g][:, cols, :].rearrange("p j t -> p (j t)"),
                    )

        late_s = keep.tile([P, GROUPS * H + PICK], U8, name="late_s", tag="last", align_bytes=64)
        w2_s = late_s[:, : GROUPS * H].rearrange("p (b n) -> p b n", b=GROUPS)
        x_s = [late_s[:, GROUPS * H :], x_s1[:]]
        nc.vector.quantize_mx(out=x_w[0][:].bitcast(FP8X4), scales=x_s[0], in_=x_b[0][:].rearrange("p j t -> p (j t)"))
        for b, g in chunks:
            cols = slice(g * GROUP, (g + 1) * GROUP)
            nc.vector.quantize_mx(out=w2_w[:, b, cols].bitcast(FP8X4), scales=w2_s[:, b, cols], in_=w2_b[b][g][:])

        def product(acc, stationary, moving):
            for b in range(GROUPS):
                (l_w, l_s), (r_w, r_s) = stationary(b), moving(b)
                nc.tensor.matmul_mx(
                    out=acc[:],
                    lhsT=l_w.bitcast(FP8X4),
                    lhsT_scale=l_s,
                    rhs=r_w.bitcast(FP8X4),
                    rhs_scale=r_s,
                    start=(b == 0),
                    stop=(b == GROUPS - 1),
                )

        direct = []
        for t in range(PACK):
            acc = psum.tile([P, PICK], F32, name=f"sum{t}", tag=f"bank{t}")
            cols = slice(t * P, (t + 1) * P)
            product(acc, lambda b: (w2_w[:, b, cols], w2_s[:, b, cols]), lambda b: (x_w[b][:], x_s[b]))
            direct.append(acc)
        sums_t = keep.tile([P, BLOCKS, PACK, P], F32, name="sums_t", tag="table1", align_bytes=64)
        for c in range(BLOCKS):
            acc = psum.tile([P, GROUP], F32, name=f"sum_t{c}", tag=f"bank{BLOCKS + c}")
            cols = slice(c * P, (c + 1) * P)
            product(acc, lambda b: (x_w[b][:, cols], x_s[b][:, cols]), lambda b: (w2_w[:, b, GROUP:], w2_s[:, b, GROUP:]))
            nc.scalar.copy(out=sums_t[:, c, :, :], in_=acc[:].rearrange("p (m t) -> p t m", t=PACK))

        for g in range(GROUPS):
            y = keep.tile([P, PACK, PICK], F32, name=f"y{g}", tag=f"rows{g}")
            y_b = keep.tile([P, PICK, PACK], BF16, name=f"y_b{g}", tag="table1" if g == 0 else "rounded01", align_bytes=64)
            for t in range(PACK):
                s = g * PACK + t
                scale = dn_t[:, g, t : t + 1]
                if g == 0:
                    nc.vector.scalar_tensor_tensor(
                        out=firm[g][:, t, :], in0=direct[t][:], scalar=scale, in1=firm[g][:, t, :], op0=MULT, op1=ADD
                    )
                else:
                    back = psum.tile([P, BLOCKS, P], F32, name=f"back{t}", tag=f"bank{t}")
                    for c in range(BLOCKS):
                        for term, first in ((bulk_t, True), (sums_t, False)):
                            nc.tensor.matmul(
                                back[:, c, :], term[:, c, t, :], ident[:], start=first, stop=not first, is_transpose=True
                            )
                    nc.scalar.activation(
                        out=firm[g][:, t, :], in_=back[:].rearrange("p c j -> p (c j)"), func=ACT.Copy, scale=scale
                    )
                halves = pieces(2 if s == SLICES - 1 else 1, PICK)
                for i, (cols, part) in enumerate(halves):
                    nc.vector.tensor_tensor(
                        out=y[:, t, cols], in0=page[s][:].indirect(list4[:, part]), in1=firm[g][:, t, cols], op=MULT
                    )
                    nc.sync.dma_start(out=dealt(out_0, g)[:, t, cols], in_=y[:, t, cols])
                    if t == PACK - 1:
                        rounded = y_b[:, cols, :].rearrange("p (c n) t -> p c t n", n=RUN)
                        exact = y[:, :, cols].rearrange("p t (c n) -> p c t n", n=RUN)
                        if i == 0:
                            nc.scalar.copy(out=rounded, in_=exact)
                        else:
                            nc.vector.tensor_copy(out=rounded, in_=exact)
            nc.vector.quantize_mx(out=y_w[g][:].bitcast(FP8X4), scales=y_s[g][:], in_=y_b[:].rearrange("p j t -> p (j t)"))
            nc.sync.dma_start(out=out_1[g].rearrange("p m t -> p (m t)").bitcast(I32), in_=y_w[g][:].bitcast(I32))
            for q in range(QUADS):
                queue = nc.scalar if q % 2 else nc.sync
                queue.dma_start(
                    out=out_2[g].bitcast(I32)[4 * q : 4 * q + 4, :], in_=y_s[g][QUAD * q : QUAD * q + 4, :].bitcast(I32)
                )
